import numpy as np, ml_dtypes
CORES = [48,51,52,55]
N = 4
BF = ml_dtypes.bfloat16
def f(rng, *shape):
    return (rng.standard_normal(shape, dtype=np.float32) * np.exp2(rng.integers(-2, 3, shape[:-1] + (1,)))).astype(BF)
def wide(rng, *shape):
    v = f(rng, *shape).astype(np.float32); k = shape[:-2] + (1, shape[-1])
    return (v * np.exp2(rng.integers(-6, 7, k)) * (rng.random(k) > 0.0625)).astype(BF)
def gentries(a):
    return np.ascontiguousarray(a.reshape(8, 16, -1).transpose(0, 2, 1)).reshape(8, -1)
def gtable(e):
    e = np.asarray(e); return np.ascontiguousarray(e.reshape(8, -1, 16).transpose(0, 2, 1)).reshape(128, -1).astype(np.int32)
Q, CAPP, M, E, D = 256, 80, 3072, 6144, 5
LV, L = [1, 5, 40, 260, 1500], 3000
EMPTY = 2 ** 24 - 1
def cut(rng, n, m, cap, s):
    u = rng.random((m, cap - 1)) + s * rng.random((m, 1))
    return 1 + np.bincount(np.argsort(u.reshape(-1))[:n - m] // (cap - 1), minlength=m)
def tree(rng, lv, n, keys, repeat=False):
    nk = np.sort(rng.integers(0, EMPTY - 16, (16, M)), axis=0) + np.arange(16)[:, None]
    nk[np.arange(16)[:, None] >= rng.integers(1, 17, (1, M))] = EMPTY
    beg = rng.integers(0, E - 15, M); kid = rng.integers(0, M, E)
    ids = np.concatenate([[0], 1 + rng.permutation(M - 1)]); a = np.cumsum([0] + list(lv))
    lev = [ids[a[l]:a[l + 1]] for l in range(D)]; nxt = lev[1:] + [rng.integers(0, M, n) if repeat else rng.permutation(M)[:n]]
    ek = np.asarray(keys); sizes = []
    for l in range(D - 1, -1, -1):
        sz = cut(rng, len(ek), lv[l], 16, 2.0); st = np.cumsum(sz) - sz
        nk[:, lev[l]] = EMPTY; nk[np.arange(len(ek)) - np.repeat(st, sz), np.repeat(lev[l], sz)] = ek
        ek = ek[st]; sizes.insert(0, sz)
    S = np.concatenate(sizes); C = np.concatenate(nxt); t = len(C); m = len(S)
    o = rng.permutation(m); so = S[o]; st = np.zeros(m, np.int64)
    st[o] = np.cumsum(so) - so + np.sort(rng.integers(0, E - 16 - t + 1, m))
    beg[ids[:m]] = st; kid[np.repeat(st - (np.cumsum(S) - S), S) + np.arange(t)] = C
    return nk, beg, kid
def make(rng, shapes=None, ends=False, full=False, alike=False, repeat=False):
    shapes = shapes or [(LV, L)] * N; I = np.int32
    spl = np.sort(rng.integers(0, EMPTY - 16384 * N + 1, (8, N - 1)), axis=1) + 16384 * np.arange(1, N)
    spl = np.concatenate([np.zeros((8, 1), np.int64), spl], axis=1); hi = np.concatenate([spl[:, 1:], np.full((8, 1), EMPTY)], axis=1)
    nk = np.zeros((N, 128, M), I); beg = np.zeros((N, 8, M), I); kid = np.zeros((N, 8, E), I); sk = np.zeros((N, 8, M), np.int64); ln = np.array([n for _, n in shapes])
    for r in range(N):
        lv, n = shapes[r]
        for g in range(8):
            w = int(hi[g, r] - spl[g, r])
            if ends: k = np.arange(n) + (w - n) * (r % 2)
            else: k = np.sort(rng.integers(0, w - n + 1, n)) + np.arange(n)
            k[0] = 0; k = k + spl[g, r]; sk[r, g, :n] = k
            nk[r, 16 * g:16 * g + 16], beg[r, g], kid[r, g] = tree(rng, lv, n, k, repeat)
    q = np.zeros((N, 8, Q), np.int64)
    for r in range(N):
        for g in range(8):
            if full: cn = np.zeros(N, np.int64); cn[rng.permutation(N)] = np.clip(Q - CAPP * np.arange(N), 0, CAPP)
            else: cn = 3 + cut(rng, Q - 3 * N, N, CAPP - 3, 0.5)
            own = np.repeat(np.arange(N), cn); st = np.cumsum(cn) - cn; occ = np.arange(Q) - st[own]
            a = spl[g, own]; b = hi[g, own]; k = sk[own, g, np.floor(rng.random(Q) * ln[own]).astype(np.int64)]
            inside = a + np.floor(rng.random(Q) * (b - a)).astype(np.int64)
            kd = 1 + occ % 4 if ends else np.array([0, 0, 0, 0, 0, 1, 1, 1, 2, 2, 2, 3, 4])[rng.integers(0, 13, Q)]
            v = np.choose(kd, [inside, k, np.maximum(k - 1, a), a, b - 1])
            if alike: v = v[st[own]]
            q[r, g] = v[rng.permutation(Q)]
    return {"nk": nk, "beg": beg, "kid": kid, "vec": f(rng, N, 128, M), "spl": np.stack([spl.astype(I)] * N), "q": np.stack([gtable(x) for x in q])}
def setup_inputs(rng):
    return make(rng)
def setup_inputs_caps(rng):
    return make(rng, full=True)
def setup_inputs_ends(rng):
    return make(rng, ends=True)
def setup_inputs_shapes(rng):
    a = []; n = M
    for l in range(D): n = -(-n // 16); a.insert(0, n)
    k = M * 3 // 8; b = [min(16 ** l, k) for l in range(D)]; s = int(rng.integers(0, 2))
    return make(rng, shapes=[(a, M) if (r + s) % 2 else (b, k) for r in range(N)], repeat=True)
def setup_inputs_alike(rng):
    return make(rng, alike=True)
def setup_inputs_spread(rng):
    d = make(rng); d["vec"] = wide(rng, N, 128, M); return d
def check_inputs(d):
    bad = []; nk, beg, kid, spl, q = [np.asarray(d[x]).astype(np.int64) for x in ("nk", "beg", "kid", "spl", "q")]
    if not np.isfinite(np.asarray(d["vec"]).astype(np.float32)).all(): bad.append("finite")
    if any(bool((a < 0).any() or (a > b).any()) for a, b in ((nk, EMPTY), (beg, E - 16), (kid, M - 1), (spl, EMPTY - 1), (q, EMPTY - 1))): return bad + ["ranges"]
    if (spl != spl[:1]).any() or (spl[:, :, 0] != 0).any() or (np.diff(spl, axis=2) <= 0).any(): return bad + ["splitters"]
    n4 = nk.reshape(N, 8, 16, M)
    if ((n4[:, :, 1:] <= n4[:, :, :-1]) & (n4[:, :, 1:] < EMPTY)).any(): bad.append("nodes")
    ok = True
    for r in range(N):
        for g in range(8):
            nd = np.zeros(1, np.int64); ek = spl[r, g, r:r + 1]; seen = [nd]
            for l in range(D):
                k = n4[r, g][:, nd].T
                if len(nd) > M or (k[:, 0] != ek).any(): ok = False; break
                use = k < EMPTY; ek = k[use]; nd = kid[r, g][(beg[r, g][nd][:, None] + np.arange(16))[use]]
                if l < D - 1:
                    seen.append(nd)
                    if len(nd) > M: ok = False; break
            if not ok: break
            s = np.concatenate(seen); top = spl[r, g, r + 1] if r + 1 < N else EMPTY
            if len(np.unique(s)) != len(s) or (np.diff(ek) <= 0).any() or ek[-1] >= top: ok = False
        if not ok: break
    if not ok: bad.append("tree")
    for r in range(N):
        x = gentries(q[r]); own = np.sum(x[:, :, None] >= spl[r][:, None, :], axis=2) - 1
        if any(np.bincount(own[g], minlength=N).max() > CAPP for g in range(8)): bad.append("caps"); break
    return bad
def reference(nk, beg, kid, vec, spl, q):
    y = np.zeros((N, 128, Q), vec.dtype); G = np.arange(8)[:, None]
    n4 = nk.reshape(N, 8, 16, M); v4 = vec.reshape(N, 8, 16, M)
    for r in range(N):
        x = gentries(q[r])
        own = np.sum(x[:, :, None] >= spl[r][:, None, :], axis=2) - 1
        at = np.zeros((8, Q), np.int64)
        for l in range(D):
            c = np.sum(n4[own, G, :, at] <= x[:, :, None], axis=2)
            at = kid[own, G, beg[own, G, at] + c - 1]
        y[r] = v4[own, G, :, at].transpose(0, 2, 1).reshape(128, Q)
    return {"y": y}

@@ -1,0 +1,352 @@
+from concourse.bass import DstId, RemoteDMATransfer
+from concourse.mybir import AluOpType as A, ActivationFunctionType as AF
+
+CAP = 80
+NS = 4 * CAP
+FILL = 16777214
+NKA, NKB = 1536, 2304
+
+SCRATCH = {
+    "x": ("sbuf", [128, 256], "int32"),
+    "xq": ("sbuf", [128, 560], "int32"),
+    "ansb": ("sbuf", [128, 560], "bfloat16"),
+    "yb": ("sbuf", [128, 256], "bfloat16"),
+    "nks": ("sbuf", [128, 3072], "int32"),
+    "vecs": ("sbuf", [128, 3072], "bfloat16"),
+    "TB": ("sbuf", [128, 6144], "bfloat16"),
+    "kidc": ("sbuf", [128, 384], "int32"),
+    "begc": ("sbuf", [128, 192], "int32"),
+    "khi": ("sbuf", [128, 384], "bfloat16"),
+    "klo": ("sbuf", [128, 384], "bfloat16"),
+    "bhi": ("sbuf", [128, 192], "bfloat16"),
+    "blo": ("sbuf", [128, 192], "bfloat16"),
+    "Z": ("sbuf", [128, 256], "bfloat16"),
+    "row": ("sbuf", [128, 144], "float32"),
+    "qg": ("sbuf", [128, 128], "float32"),
+    "sel": ("sbuf", [128, 128], "float32"),
+    "Id16": ("sbuf", [128, 128], "float32"),
+    "s2f": ("sbuf", [128, 20], "float32"),
+    "m2b": ("sbuf", [128, 16], "bfloat16"),
+    "bm": ("sbuf", [128, 16], "bfloat16"),
+    "nk2": ("sbuf", [128, 16], "int32"),
+    "nk3": ("sbuf", [128, 256], "int32"),
+}
+for _n in ("pid", "oi", "gi", "spli"):
+    SCRATCH[_n] = ("sbuf", [128, 8], "int32")
+for _n in ("w", "wa", "wb", "pidf", "icol", "gcol", "g16", "m0", "m2c", "mB", "big", "thr", "rootc", "splf"):
+    SCRATCH[_n] = ("sbuf", [128, 8], "float32")
+for _n in ("F", "FW", "FK", "FB"):
+    SCRATCH[_n] = ("sbuf", [128, 144], "bfloat16")
+for _n in ("Dm", "Id", "Ball", "BallB", "R0", "km"):
+    SCRATCH[_n] = ("sbuf", [128, 128], "bfloat16")
+for _n in ("geo", "H", "prod", "kg3", "bl3"):
+    SCRATCH[_n] = ("sbuf", [128, 256], "bfloat16")
+for _n in ("posS", "posG", "e1", "ml2", "e2", "ml3"):
+    SCRATCH[_n] = ("sbuf", [128, 16], "uint16")
+for _n in ("s2", "s3", "e3", "n4", "e4", "n5", "e5", "vl"):
+    SCRATCH[_n] = ("sbuf", [128, 20], "uint16")
+for _n in ("ge1", "ge2", "ge3", "ge4", "ge5", "kg4", "kg5", "kg6", "bp3", "bp4", "bp5"):
+    SCRATCH[_n] = ("sbuf", [128, NS], "bfloat16")
+for _n in range(8):
+    SCRATCH["p%d" % _n] = ("psum", [128, 512], "float32")
+
+SEMAPHORES = ["arrx", "arry", "lsx", "lsy", "xl", "sent"] + ["e%d" % _k for _k in range(144)]
+
+
+def rank_program(g, core, T, topo):
+    own = T.rank_of(core)
+    if own is None:
+        return
+    N = 4
+    V, S, P, Y = g.vector, g.scalar, g.tensor, g.sync
+    used = [0]
+    done = {"v": {}, "s": {}, "p": {}, "y": {}, "g": {}}
+    names = (("v", V), ("s", S), ("p", P), ("y", Y), ("g", g))
+
+    def ev(inst, n=1):
+        k = "e%d" % used[0]
+        used[0] += 1
+        inst.then_inc(T.sem[k], n)
+        return (k, n)
+
+    def dm(inst):
+        return ev(inst, 16)
+
+    def wait(q, *events):
+        for name, queue in names:
+            if name == q:
+                for k, n in events:
+                    if done[q].get(k, 0) < n:
+                        queue.wait_ge(T.sem[k], n)
+                        done[q][k] = n
+
+    def collect(ps, n, terms, first=True):
+        tot = 16 * len(terms)
+        k = 0
+        last = None
+        for fb, rhs, stepped, events in terms:
+            wait("p", *events)
+            for i in range(16):
+                r = rhs[:, i:16 * n:16] if stepped else rhs[:, 16 * i:16 * i + n]
+                last = P.matmul(ps[:, 0:n], fb[:, 16 - i:144 - i], r, first and k == 0, k == tot - 1)
+                k += 1
+        return ev(last)
+
+    def halves(ps, terms):
+        tot = 8 * len(terms)
+        k = 0
+        last = None
+        for fb, rhs, h, events in terms:
+            wait("p", *events)
+            for i in range(8):
+                last = P.matmul(ps[:, 0:20], fb[:, 16 - 8 * h - i:144 - 8 * h - i], rhs[:, 160 * h + i:160 * h + 160:8],
+                                k == 0, k == tot - 1)
+                k += 1
+        return ev(last)
+
+    e_beg = dm(S.dma_start(T.begc[:], T.beg[:]))
+    e_spl = dm(Y.dma_start(T.spli[0:32, 0:1], T.spl[:]))
+    for o in range(16):
+        q = Y if o % 2 == 0 else S
+        q.dma_start(T.x[o::16, :], T.q[:]).then_inc(T.sem.xl, 16)
+    e_x = ("xl", 256)
+    e_kid = dm(S.dma_start(T.kidc[:], T.kid[:]))
+    e_nk = [dm(Y.dma_start(T.nks[:, 0:NKA], T.nk[:, 0:NKA]))]
+
+    z = ev(V.memset(T.Dm[:], 0.0))
+    z2 = ev(V.memset(T.sel[0:32, :], 0.0))
+    f1 = ev(V.memset(T.TB[:, 0:1792], 0.0))
+    i_pid = ev(g.iota(T.pid[:, 0:1], [[1, 1]], 0, 1))
+    i_row = ev(g.iota(T.row[:], [[1, 144]], 0, 0, allow_small_or_imprecise_dtypes=True))
+    wait("g", z2)
+    c_sel = ev(g.affine_select(T.sel[0:32, :], T.sel[0:32, :], [[-4, 8], [-1, 16]], A.not_equal, 1.0, 0, 1))
+    c_D = z
+    for step, fill, base in (([[-1, 128]], 2.0, 0), ([[-1, 128]], -1.0, -1), ([[-1, 128]], -1.0, 1),
+                             ([[-16, 8], [-1000, 16]], 1.0, 0)):
+        wait("g", c_D)
+        c_D = ev(g.affine_select(T.Dm[:], T.Dm[:], step, A.not_equal, fill, base, 1))
+    i_qg = ev(g.iota(T.qg[:], [[1, 8], [0, 16]], 0, 0, allow_small_or_imprecise_dtypes=True))
+    fx = ev(g.iota(T.xq[:, 240:560], [[0, 320]], FILL, 0))
+    f4 = ev(g.iota(T.TB[:, 5760:6144], [[0, 384]], 0, 0, allow_small_or_imprecise_dtypes=True))
+
+    zs = ev(V.memset(T.Z[:], 0.0))
+    wait("v", i_pid)
+    c_o = ev(V.tensor_scalar(T.oi[:, 0:1], T.pid[:, 0:1], 15, None, A.bitwise_and))
+    c_g = ev(V.tensor_scalar(T.gi[:, 0:1], T.pid[:, 0:1], 4, None, A.arith_shift_right))
+    c_pf = ev(V.tensor_copy(T.pidf[:, 0:1], T.pid[:, 0:1]))
+    f3 = ev(V.memset(T.TB[:, 5376:5760], 0.0))
+    wait("v", c_o, c_g)
+    c_g16 = ev(V.tensor_scalar(T.g16[:, 0:1], T.gi[:, 0:1], 16.0, 16.0, A.mult, A.add))
+    c_big = ev(V.tensor_scalar(T.big[:, 0:1], T.oi[:, 0:1], 4.0, 33554432.0, A.is_ge, A.mult))
+    c_wa = ev(V.tensor_scalar(T.wa[:, 0:1], T.oi[:, 0:1], float(own), -4.0 * CAP, A.is_equal, A.mult))
+    c_wb = ev(V.tensor_scalar(T.wb[:, 0:1], T.oi[:, 0:1], 0.0, float(CAP * (N - 1 - own)), A.is_equal, A.mult))
+    wait("v", c_pf, i_row)
+    c_Id = ev(V.tensor_scalar(T.Id[:], T.row[:, 0:128], T.pidf[:, 0:1], None, A.is_equal))
+    wait("v", c_g16)
+    c_F = ev(V.tensor_scalar(T.F[:], T.row[:], T.g16[:, 0:1], None, A.is_equal))
+    wait("v", c_wa, c_wb)
+    c_w = ev(V.tensor_scalar(T.w[:, 0:1], T.wa[:, 0:1], float(CAP), T.wb[:, 0:1], A.add, A.add))
+    wait("v", e_spl)
+    c_sf = ev(V.tensor_copy(T.splf[0:32, 0:1], T.spli[0:32, 0:1]))
+    wait("p", c_sf, c_sel)
+    p_thr = ev(P.matmul(T.p0[:, 0:1], T.sel[0:32, :], T.splf[0:32, 0:1], True, True))
+    wait("v", e_beg)
+    b_hi = ev(V.tensor_copy(T.bhi[:], T.begc[:]))
+    wait("p", c_Id, b_hi)
+    b_ps = ev(P.matmul(T.p6[:, 0:192], T.Id[:], T.bhi[:], True, True))
+    wait("v", c_F, c_w)
+    c_FW = ev(V.tensor_scalar(T.FW[:], T.F[:], T.w[:, 0:1], None, A.mult))
+    wait("v", p_thr, c_big)
+    c_thr = ev(V.tensor_scalar(T.thr[:, 0:1], T.p0[:, 0:1], T.big[:, 0:1], None, A.add))
+    wait("v", b_ps)
+    b_lo = ev(V.tensor_tensor(T.blo[:], T.begc[:], T.p6[:, 0:192], A.subtract))
+
+    wait("s", f1)
+    f2 = [ev(S.activation(T.TB[:, 1792:3584], T.TB[:, 0:1792], AF.Copy))]
+    f2.append(ev(S.activation(T.TB[:, 3584:5376], T.TB[:, 0:1792], AF.Copy)))
+
+    wait("v", e_x, c_thr)
+    r_ge = ev(V.tensor_scalar(T.geo[:], T.x[:], T.thr[:, 0:1], None, A.is_ge))
+    wait("v", zs, r_ge)
+    r_h = ev(V.tensor_tensor_scan(T.H[:], T.geo[:], T.Z[:], 0.0, A.add, A.add))
+    wait("p", c_FW, r_ge)
+    for i in range(4):
+        P.matmul(T.p2[:, 0:16], T.FW[:, 16 - i:144 - i], T.geo[:, i:256:16], i == 0, False)
+    wait("p", c_D, r_h)
+    r_oh = ev(P.matmul(T.p1[:, 0:256], T.Dm[:], T.H[:], True, True))
+    wait("v", e_kid)
+    k_hi = ev(V.tensor_copy(T.khi[:], T.kidc[:]))
+    wait("v", r_oh)
+    r_pr = ev(V.tensor_tensor(T.prod[:], T.p1[:, 0:256], T.geo[:], A.mult))
+    for i in range(4, 16):
+        P.matmul(T.p2[:, 0:16], T.FW[:, 16 - i:144 - i], T.geo[:, i:256:16], False, False)
+    wait("p", k_hi)
+    k_ps = ev(P.matmul(T.p7[:, 0:384], T.Id[:], T.khi[:], True, True))
+    r_ps = collect(T.p2, 16, [(T.F, T.prod, True, [c_F, r_pr])], False)
+    r_pg = collect(T.p3, 16, [(T.FW, T.geo, False, []), (T.F, T.prod, False, [])])
+    c_gc = ev(V.tensor_copy(T.gcol[:, 0:1], T.gi[:, 0:1]))
+    c_m0 = ev(V.tensor_scalar(T.m0[:, 0:1], T.oi[:, 0:1], 0.0, None, A.is_equal))
+    c_i = ev(V.tensor_copy(T.icol[:, 0:1], T.oi[:, 0:1]))
+    wait("v", k_ps)
+    k_lo = ev(V.tensor_tensor(T.klo[:], T.kidc[:], T.p7[:, 0:384], A.subtract))
+    wait("v", i_qg, c_gc)
+    c_B = ev(V.tensor_scalar(T.Ball[:], T.qg[:], T.gcol[:, 0:1], None, A.is_equal))
+    wait("v", r_ps)
+    r_pos = ev(V.tensor_scalar(T.posS[:], T.p2[:, 0:16], -1.0, None, A.add))
+    wait("v", r_pos, fx)
+    r_sc = ev(V.tensor_copy(T.xq[:, 240:560].indirect(T.posS[:, 0:16]), T.x[:]))
+
+    c_m2 = ev(V.tensor_scalar(T.m2c[:, 0:1], T.oi[:, 0:1], 2.0, None, A.is_lt))
+    c_mB = ev(V.tensor_scalar(T.mB[:, 0:1], T.oi[:, 0:1], 14.0, None, A.is_ge))
+    wait("s", c_B, c_m0)
+    c_R0 = ev(S.activation(T.R0[:], T.Ball[:], AF.Identity, scale=T.m0[:, 0:1]))
+    wait("s", c_m2)
+    c_mb = ev(S.activation(T.m2b[:, 0:1], T.m2c[:, 0:1], AF.Copy))
+    wait("s", c_mB)
+    c_BB = ev(S.activation(T.BallB[:], T.Ball[:], AF.Identity, scale=T.mB[:, 0:1]))
+    c_FK = ev(S.activation(T.FK[:], T.F[:], AF.Identity, scale=T.m2c[:, 0:1]))
+    c_FB = ev(S.activation(T.FB[:], T.F[:], AF.Identity, scale=T.mB[:, 0:1]))
+    c_I16 = ev(S.activation(T.Id16[:], T.Id[:], AF.Copy, scale=16.0))
+
+    near = [r for r in range(N) if r != own and topo.die(T.cores[r]) == topo.die(core)]
+    far = [r for r in range(N) if r != own and topo.die(T.cores[r]) != topo.die(core)]
+    masks = {}
+    for k, r in enumerate(far):
+        masks[r] = topo.engines(core, T.cores[r])[0::2][4 * k:4 * k + 4]
+    for k, r in enumerate(near):
+        masks[r] = topo.engines(core, T.cores[r])[1::2][4 * k:4 * k + 4]
+
+    def send(buf, sb, db, sem, lsem):
+        tr = []
+        for r in far + near:
+            rid, pid, _s = topo.addr(T.cores[r])
+            a, b = sb(r), db(r)
+            tr.append(RemoteDMATransfer(dst_ids=[DstId(rid=rid, pnc=pid)], dma_engine_mask=sum(1 << e for e in masks[r]),
+                                        remote_sem=sem, src=buf[:, a:a + CAP], dst=buf[:, b:b + CAP]))
+        g.remote_dma_fused(tr, local_sem=lsem)
+
+    wait("g", r_sc)
+    send(T.xq, lambda r: 240 + CAP * ((r - own) % N), lambda r: CAP * ((own - r) % N - 1), T.sem.arrx, T.sem.lsx)
+    a_x = ("arrx", 12)
+    g.sem_inc(T.sem.sent, 1)
+
+    wait("y", b_hi, b_lo, f1, f3, f4, *f2)
+    t_b = dm(Y.dma_start(T.TB[14::16, 0:3072], T.bhi[:]))
+    t_c = dm(Y.dma_start(T.TB[15::16, 0:3072], T.blo[:]))
+    wait("y", k_hi, k_lo)
+    t_k = dm(Y.dma_start(T.TB[0::16, :], T.khi[:]))
+    t_l = dm(Y.dma_start(T.TB[1::16, :], T.klo[:]))
+    e_nk.append(dm(Y.dma_start(T.nks[:, NKA:NKB], T.nk[:, NKA:NKB])))
+    wait("y", ("sent", 1))
+    e_nk.append(dm(Y.dma_start(T.nks[:, NKB:3072], T.nk[:, NKB:3072])))
+    e_vec = dm(Y.dma_start(T.vecs[:], T.vec[:]))
+    tb = [t_k, t_l, t_b, t_c]
+
+    X = T.xq[:, 0:NS]
+    wait("p", c_R0, b_hi, b_lo)
+    P.matmul(T.p4[:, 0:1], T.R0[:], T.bhi[:, 0:1], True, False)
+    d0 = ev(P.matmul(T.p4[:, 0:1], T.R0[:], T.blo[:, 0:1], False, True))
+    wait("v", d0, c_i)
+    d1 = ev(V.tensor_scalar(T.e1[:, 0:8], T.Z[:, 0:8], T.p4[:, 0:1], T.icol[:, 0:1], A.add, A.add))
+    wait("v", d1, *tb)
+    d2 = ev(V.tensor_tensor(T.km[:], T.TB[:].indirect(T.e1[:, 0:8]), T.Ball[:], A.mult))
+    wait("p", c_mb, d2)
+    d3 = ev(P.matmul(T.p5[:, 0:1], T.km[:], T.m2b[:, 0:1], True, True))
+    wait("v", d3)
+    d4 = ev(V.tensor_copy(T.ml2[:, 0:1], T.p5[:, 0:1]))
+    wait("v", d4)
+    d5 = ev(V.tensor_copy(T.bm[:], T.TB[:, 0:3072].indirect(T.ml2[:, 0:1])))
+    wait("p", c_BB, d5)
+    d6 = ev(P.matmul(T.p6[:, 0:16], T.BallB[:], T.bm[:], True, True))
+    wait("v", r_pg)
+    r_posg = ev(V.tensor_scalar(T.posG[:], T.p3[:, 0:16], -1.0, None, A.add))
+    wait("v", e_nk[0])
+    c_rt = ev(V.tensor_copy(T.rootc[:, 0:1], T.nks[:, 0:1]))
+
+    def to_list(buf, ps, event, add):
+        wait("v", event)
+        e = ev(V.tensor_scalar(buf[:], ps[:, 0:20], float(add), None, A.add))
+        wait("v", e)
+        return e
+
+    def two_lists(buf, ps, event, add):
+        wait("v", event)
+        return [ev(V.tensor_scalar(buf[:, 10 * p:10 * p + 10], ps[:, p:20:2], float(add), None, A.add)) for p in range(2)]
+
+    def level(keys, starts, lst, el, ge, bp, ps, deps_v, deps_s):
+        wait("s", el[0], *deps_s)
+        ea = ev(S.activation(bp[:, 64:160], starts.indirect(lst[:, 4:10]), AF.Copy))
+        wait("v", el[0], *deps_v, *deps_s)
+        eb = ev(V.tensor_copy(bp[:, 0:64], starts.indirect(lst[:, 0:4])))
+        g0 = ev(V.tensor_tensor(ge[:, 0:160], keys.indirect(lst[:, 0:10]), T.xq[:, 0:160], A.is_le))
+        wait("s", el[1])
+        ec = ev(S.activation(bp[:, 160:320], starts.indirect(lst[:, 10:20]), AF.Copy))
+        wait("v", el[1])
+        g1 = ev(V.tensor_tensor(ge[:, 160:320], keys.indirect(lst[:, 10:20]), T.xq[:, 160:320], A.is_le))
+        return halves(ps, [(T.FB, bp, 0, [c_FB, ea, eb]), (T.F, ge, 0, [g0]), (T.FB, bp, 1, [ec]), (T.F, ge, 1, [g1])])
+
+    def child(lst, el, kg, ps):
+        ee = []
+        for h, va in enumerate((6, 4)):
+            c = 10 * h
+            wait("s", el[h])
+            a = ev(S.activation(kg[:, 16 * (c + va):16 * (c + 10)], T.TB[:].indirect(lst[:, c + va:c + 10]), AF.Copy))
+            wait("v", el[h])
+            b = ev(V.tensor_copy(kg[:, 16 * c:16 * (c + va)], T.TB[:].indirect(lst[:, c:c + va])))
+            ee.append([a, b])
+        return halves(ps, [(T.FK, kg, 0, [c_FK] + ee[0]), (T.FK, kg, 1, ee[1])])
+
+    wait("v", r_sc, c_rt)
+    w0 = ev(V.tensor_scalar(T.ge1[:, 240:320], T.xq[:, 240:320], T.rootc[:, 0:1], None, A.is_ge))
+    wait("v", a_x)
+    w1 = ev(V.tensor_scalar(T.ge1[:, 0:240], T.xq[:, 0:240], T.rootc[:, 0:1], None, A.is_ge))
+    q1 = collect(T.p5, 20, [(T.F, T.ge1, True, [c_F, w0, w1])])
+    wait("v", d6)
+    d7 = ev(V.tensor_scalar(T.e2[:], T.p6[:, 0:16], T.icol[:, 0:1], None, A.add))
+    wait("v", d7)
+    d8 = ev(V.tensor_copy(T.kg3[:, 0:128], T.TB[:].indirect(T.e2[:, 0:8])))
+    wait("s", d7, *tb)
+    d9 = ev(S.activation(T.kg3[:, 128:256], T.TB[:].indirect(T.e2[:, 8:16]), AF.Copy))
+    d10 = collect(T.p4, 16, [(T.FK, T.kg3, True, [c_FK, d8, d9])])
+    wait("v", *e_nk)
+    d11 = ev(V.tensor_copy(T.nk2[:], T.nks[:].indirect(T.ml2[:, 0:1])))
+    s2 = to_list(T.s2, T.p5, q1, -1)
+    wait("s", s2)
+    s2f = ev(S.activation(T.s2f[:], T.p5[:, 0:20], AF.Copy))
+    wait("v", d11)
+    w2 = ev(V.tensor_tensor(T.ge2[:], T.nk2[:].indirect(T.s2[:]), X, A.is_le))
+    wait("p", s2f, c_I16)
+    P.matmul(T.p6[:, 0:20], T.Id16[:], T.s2f[:], True, False)
+    q2 = collect(T.p6, 20, [(T.F, T.ge2, True, [w2])], False)
+    wait("v", d10)
+    d12 = ev(V.tensor_copy(T.ml3[:], T.p4[:, 0:16]))
+    wait("s", d12)
+    d14 = ev(S.activation(T.bl3[:], T.TB[:, 0:3072].indirect(T.ml3[:]), AF.Copy))
+    wait("v", d12)
+    d13 = ev(V.tensor_copy(T.nk3[:], T.nks[:].indirect(T.ml3[:])))
+    s3 = to_list(T.s3, T.p6, q2, -17)
+    e3 = two_lists(T.e3, T.p4, level(T.nk3[:], T.bl3[:], T.s3, [s3, s3], T.ge3, T.bp3, T.p4, [d13], [d14]), -1)
+    n4 = two_lists(T.n4, T.p5, child(T.e3, e3, T.kg4, T.p5), 0)
+    e4 = two_lists(T.e4, T.p6, level(T.nks[:], T.TB[:, 0:3072], T.n4, n4, T.ge4, T.bp4, T.p6, [], []), -1)
+    n5 = two_lists(T.n5, T.p4, child(T.e4, e4, T.kg5, T.p4), 0)
+    e5 = two_lists(T.e5, T.p5, level(T.nks[:], T.TB[:, 0:3072], T.n5, n5, T.ge5, T.bp5, T.p5, [], []), -1)
+    vl = two_lists(T.vl, T.p6, child(T.e5, e5, T.kg6, T.p6), 0)
+
+    wait("v", e_vec, vl[0])
+    va = ev(V.tensor_copy(T.ansb[:, 0:128], T.vecs[:].indirect(T.vl[:, 0:8])))
+    wait("s", e_vec, *vl)
+    vb = ev(S.activation(T.ansb[:, 128:256], T.vecs[:].indirect(T.vl[:, 8:16]), AF.Copy))
+    wait("v", vl[1])
+    vc = ev(V.tensor_copy(T.ansb[:, 256:320], T.vecs[:].indirect(T.vl[:, 16:20])))
+    wait("g", va, vb)
+    send(T.ansb, lambda r: CAP * ((r - own) % N - 1), lambda r: 240 + CAP * ((own - r) % N), T.sem.arry, T.sem.lsy)
+    a_y = ("arry", 12)
+
+    wait("v", a_y, va, vb, vc, r_posg)
+    wait("s", a_y, va, vb, vc, r_posg)
+    y1 = ev(V.tensor_copy(T.yb[:, 0:128], T.ansb[:, 240:560].indirect(T.posG[:, 0:8])))
+    y2 = ev(S.activation(T.yb[:, 128:256], T.ansb[:, 240:560].indirect(T.posG[:, 8:16]), AF.Copy))
+    wait("y", y1, y2)
+    st = dm(Y.dma_start(T.y[:], T.yb[:]))
+    wait("y", st)
+    wait("g", ("lsx", 12), ("lsy", 12))

@@ -5,11 +5,14 @@ CAP = 80
 NS = 4 * CAP
 FILL = 16777214
 NKA, NKB = 1536, 2304
+ZA, ZB, ZC = 1088, 2432, 4608
 
 SCRATCH = {
     "x": ("sbuf", [128, 256], "int32"),
-    "xq": ("sbuf", [128, 560], "int32"),
-    "ansb": ("sbuf", [128, 560], "bfloat16"),
+    "W": ("sbuf", [128, NS], "int32"),
+    "X": ("sbuf", [128, NS], "int32"),
+    "An": ("sbuf", [128, NS], "bfloat16"),
+    "R": ("sbuf", [128, NS], "bfloat16"),
     "yb": ("sbuf", [128, 256], "bfloat16"),
     "nks": ("sbuf", [128, 3072], "int32"),
     "vecs": ("sbuf", [128, 3072], "bfloat16"),
@@ -20,28 +23,32 @@ SCRATCH = {
     "klo": ("sbuf", [128, 384], "bfloat16"),
     "bhi": ("sbuf", [128, 192], "bfloat16"),
     "blo": ("sbuf", [128, 192], "bfloat16"),
-    "Z": ("sbuf", [128, 256], "bfloat16"),
-    "row": ("sbuf", [128, 144], "float32"),
-    "qg": ("sbuf", [128, 128], "float32"),
+    "Z": ("sbuf", [128, 160], "bfloat16"),
+    "qq": ("sbuf", [128, 32], "int32"),
+    "qt": ("sbuf", [128, 32], "int32"),
+    "pg": ("sbuf", [128, 32], "float32"),
+    "pt": ("sbuf", [128, 32], "float32"),
+    "spli": ("sbuf", [128, 8], "int32"),
+    "splf": ("sbuf", [128, 8], "float32"),
+    "roots": ("sbuf", [128, 16], "int32"),
+    "rootf": ("sbuf", [128, 16], "float32"),
+    "mt": ("sbuf", [128, 8], "float32"),
+    "mf": ("sbuf", [128, 8], "float32"),
+    "mK": ("sbuf", [128, 16], "bfloat16"),
+    "FF": ("sbuf", [128, 432], "bfloat16"),
     "sel": ("sbuf", [128, 128], "float32"),
-    "Id16": ("sbuf", [128, 128], "float32"),
-    "s2f": ("sbuf", [128, 20], "float32"),
-    "m2b": ("sbuf", [128, 16], "bfloat16"),
+    "s2f": ("sbuf", [128, 32], "bfloat16"),
     "bm": ("sbuf", [128, 16], "bfloat16"),
     "nk2": ("sbuf", [128, 16], "int32"),
     "nk3": ("sbuf", [128, 256], "int32"),
 }
-for _n in ("pid", "oi", "gi", "spli"):
-    SCRATCH[_n] = ("sbuf", [128, 8], "int32")
-for _n in ("w", "wa", "wb", "pidf", "icol", "gcol", "g16", "m0", "m2c", "mB", "big", "thr", "rootc", "splf"):
-    SCRATCH[_n] = ("sbuf", [128, 8], "float32")
-for _n in ("F", "FW", "FK", "FB"):
-    SCRATCH[_n] = ("sbuf", [128, 144], "bfloat16")
-for _n in ("Dm", "Id", "Ball", "BallB", "R0", "km"):
+for _n in ("G", "H", "keep", "five", "prod"):
+    SCRATCH[_n] = ("sbuf", [128, 80], "bfloat16")
+for _n in ("Id", "Ball", "nBall", "U", "nU", "km"):
     SCRATCH[_n] = ("sbuf", [128, 128], "bfloat16")
-for _n in ("geo", "H", "prod", "kg3", "bl3"):
+for _n in ("kg3", "bl3"):
     SCRATCH[_n] = ("sbuf", [128, 256], "bfloat16")
-for _n in ("posS", "posG", "e1", "ml2", "e2", "ml3"):
+for _n in ("posS", "posG", "e1", "ml2", "e2", "ml3", "s2a", "s2b"):
     SCRATCH[_n] = ("sbuf", [128, 16], "uint16")
 for _n in ("s2", "s3", "e3", "n4", "e4", "n5", "e5", "vl"):
     SCRATCH[_n] = ("sbuf", [128, 20], "uint16")
@@ -50,7 +57,7 @@ for _n in ("ge1", "ge2", "ge3", "ge4", "ge5", "kg4", "kg5", "kg6", "bp3", "bp4",
 for _n in range(8):
     SCRATCH["p%d" % _n] = ("psum", [128, 512], "float32")
 
-SEMAPHORES = ["arrx", "arry", "lsx", "lsy", "xl", "sent"] + ["e%d" % _k for _k in range(144)]
+SEMAPHORES = ["arrr", "arrx", "arrl", "arry", "left", "xl", "ql", "sl", "pl", "sent"] + ["e%d" % _k for _k in range(140)]
 
 
 def rank_program(g, core, T, topo):
@@ -59,6 +66,7 @@ def rank_program(g, core, T, topo):
         return
     N = 4
     V, S, P, Y = g.vector, g.scalar, g.tensor, g.sync
+    F, FK, FB = 0, 144, 288
     used = [0]
     done = {"v": {}, "s": {}, "p": {}, "y": {}, "g": {}}
     names = (("v", V), ("s", S), ("p", P), ("y", Y), ("g", g))
@@ -68,6 +76,12 @@ def rank_program(g, core, T, topo):
         used[0] += 1
         inst.then_inc(T.sem[k], n)
         return (k, n)
+
+    def together(insts):
+        k, _n = ev(insts[0])
+        for inst in insts[1:]:
+            inst.then_inc(T.sem[k], 1)
+        return (k, len(insts))
 
     def dm(inst):
         return ev(inst, 16)
@@ -80,17 +94,12 @@ def rank_program(g, core, T, topo):
                         queue.wait_ge(T.sem[k], n)
                         done[q][k] = n
 
-    def collect(ps, n, terms, first=True):
-        tot = 16 * len(terms)
-        k = 0
+    def collect(ps, n, fb, rhs, events, close=True):
+        wait("p", *events)
         last = None
-        for fb, rhs, stepped, events in terms:
-            wait("p", *events)
-            for i in range(16):
-                r = rhs[:, i:16 * n:16] if stepped else rhs[:, 16 * i:16 * i + n]
-                last = P.matmul(ps[:, 0:n], fb[:, 16 - i:144 - i], r, first and k == 0, k == tot - 1)
-                k += 1
-        return ev(last)
+        for i in range(16):
+            last = P.matmul(ps[:, 0:n], T.FF[:, fb + 16 - i:fb + 144 - i], rhs[:, i:16 * n:16], i == 0, close and i == 15)
+        return ev(last) if close else None
 
     def halves(ps, terms):
         tot = 8 * len(terms)
@@ -99,114 +108,10 @@ def rank_program(g, core, T, topo):
         for fb, rhs, h, events in terms:
             wait("p", *events)
             for i in range(8):
-                last = P.matmul(ps[:, 0:20], fb[:, 16 - 8 * h - i:144 - 8 * h - i], rhs[:, 160 * h + i:160 * h + 160:8],
-                                k == 0, k == tot - 1)
+                a = fb + 16 - 8 * h - i
+                last = P.matmul(ps[:, 0:20], T.FF[:, a:a + 128], rhs[:, 160 * h + i:160 * h + 160:8], k == 0, k == tot - 1)
                 k += 1
         return ev(last)
-
-    e_beg = dm(S.dma_start(T.begc[:], T.beg[:]))
-    e_spl = dm(Y.dma_start(T.spli[0:32, 0:1], T.spl[:]))
-    for o in range(16):
-        q = Y if o % 2 == 0 else S
-        q.dma_start(T.x[o::16, :], T.q[:]).then_inc(T.sem.xl, 16)
-    e_x = ("xl", 256)
-    e_kid = dm(S.dma_start(T.kidc[:], T.kid[:]))
-    e_nk = [dm(Y.dma_start(T.nks[:, 0:NKA], T.nk[:, 0:NKA]))]
-
-    z = ev(V.memset(T.Dm[:], 0.0))
-    z2 = ev(V.memset(T.sel[0:32, :], 0.0))
-    f1 = ev(V.memset(T.TB[:, 0:1792], 0.0))
-    i_pid = ev(g.iota(T.pid[:, 0:1], [[1, 1]], 0, 1))
-    i_row = ev(g.iota(T.row[:], [[1, 144]], 0, 0, allow_small_or_imprecise_dtypes=True))
-    wait("g", z2)
-    c_sel = ev(g.affine_select(T.sel[0:32, :], T.sel[0:32, :], [[-4, 8], [-1, 16]], A.not_equal, 1.0, 0, 1))
-    c_D = z
-    for step, fill, base in (([[-1, 128]], 2.0, 0), ([[-1, 128]], -1.0, -1), ([[-1, 128]], -1.0, 1),
-                             ([[-16, 8], [-1000, 16]], 1.0, 0)):
-        wait("g", c_D)
-        c_D = ev(g.affine_select(T.Dm[:], T.Dm[:], step, A.not_equal, fill, base, 1))
-    i_qg = ev(g.iota(T.qg[:], [[1, 8], [0, 16]], 0, 0, allow_small_or_imprecise_dtypes=True))
-    fx = ev(g.iota(T.xq[:, 240:560], [[0, 320]], FILL, 0))
-    f4 = ev(g.iota(T.TB[:, 5760:6144], [[0, 384]], 0, 0, allow_small_or_imprecise_dtypes=True))
-
-    zs = ev(V.memset(T.Z[:], 0.0))
-    wait("v", i_pid)
-    c_o = ev(V.tensor_scalar(T.oi[:, 0:1], T.pid[:, 0:1], 15, None, A.bitwise_and))
-    c_g = ev(V.tensor_scalar(T.gi[:, 0:1], T.pid[:, 0:1], 4, None, A.arith_shift_right))
-    c_pf = ev(V.tensor_copy(T.pidf[:, 0:1], T.pid[:, 0:1]))
-    f3 = ev(V.memset(T.TB[:, 5376:5760], 0.0))
-    wait("v", c_o, c_g)
-    c_g16 = ev(V.tensor_scalar(T.g16[:, 0:1], T.gi[:, 0:1], 16.0, 16.0, A.mult, A.add))
-    c_big = ev(V.tensor_scalar(T.big[:, 0:1], T.oi[:, 0:1], 4.0, 33554432.0, A.is_ge, A.mult))
-    c_wa = ev(V.tensor_scalar(T.wa[:, 0:1], T.oi[:, 0:1], float(own), -4.0 * CAP, A.is_equal, A.mult))
-    c_wb = ev(V.tensor_scalar(T.wb[:, 0:1], T.oi[:, 0:1], 0.0, float(CAP * (N - 1 - own)), A.is_equal, A.mult))
-    wait("v", c_pf, i_row)
-    c_Id = ev(V.tensor_scalar(T.Id[:], T.row[:, 0:128], T.pidf[:, 0:1], None, A.is_equal))
-    wait("v", c_g16)
-    c_F = ev(V.tensor_scalar(T.F[:], T.row[:], T.g16[:, 0:1], None, A.is_equal))
-    wait("v", c_wa, c_wb)
-    c_w = ev(V.tensor_scalar(T.w[:, 0:1], T.wa[:, 0:1], float(CAP), T.wb[:, 0:1], A.add, A.add))
-    wait("v", e_spl)
-    c_sf = ev(V.tensor_copy(T.splf[0:32, 0:1], T.spli[0:32, 0:1]))
-    wait("p", c_sf, c_sel)
-    p_thr = ev(P.matmul(T.p0[:, 0:1], T.sel[0:32, :], T.splf[0:32, 0:1], True, True))
-    wait("v", e_beg)
-    b_hi = ev(V.tensor_copy(T.bhi[:], T.begc[:]))
-    wait("p", c_Id, b_hi)
-    b_ps = ev(P.matmul(T.p6[:, 0:192], T.Id[:], T.bhi[:], True, True))
-    wait("v", c_F, c_w)
-    c_FW = ev(V.tensor_scalar(T.FW[:], T.F[:], T.w[:, 0:1], None, A.mult))
-    wait("v", p_thr, c_big)
-    c_thr = ev(V.tensor_scalar(T.thr[:, 0:1], T.p0[:, 0:1], T.big[:, 0:1], None, A.add))
-    wait("v", b_ps)
-    b_lo = ev(V.tensor_tensor(T.blo[:], T.begc[:], T.p6[:, 0:192], A.subtract))
-
-    wait("s", f1)
-    f2 = [ev(S.activation(T.TB[:, 1792:3584], T.TB[:, 0:1792], AF.Copy))]
-    f2.append(ev(S.activation(T.TB[:, 3584:5376], T.TB[:, 0:1792], AF.Copy)))
-
-    wait("v", e_x, c_thr)
-    r_ge = ev(V.tensor_scalar(T.geo[:], T.x[:], T.thr[:, 0:1], None, A.is_ge))
-    wait("v", zs, r_ge)
-    r_h = ev(V.tensor_tensor_scan(T.H[:], T.geo[:], T.Z[:], 0.0, A.add, A.add))
-    wait("p", c_FW, r_ge)
-    for i in range(4):
-        P.matmul(T.p2[:, 0:16], T.FW[:, 16 - i:144 - i], T.geo[:, i:256:16], i == 0, False)
-    wait("p", c_D, r_h)
-    r_oh = ev(P.matmul(T.p1[:, 0:256], T.Dm[:], T.H[:], True, True))
-    wait("v", e_kid)
-    k_hi = ev(V.tensor_copy(T.khi[:], T.kidc[:]))
-    wait("v", r_oh)
-    r_pr = ev(V.tensor_tensor(T.prod[:], T.p1[:, 0:256], T.geo[:], A.mult))
-    for i in range(4, 16):
-        P.matmul(T.p2[:, 0:16], T.FW[:, 16 - i:144 - i], T.geo[:, i:256:16], False, False)
-    wait("p", k_hi)
-    k_ps = ev(P.matmul(T.p7[:, 0:384], T.Id[:], T.khi[:], True, True))
-    r_ps = collect(T.p2, 16, [(T.F, T.prod, True, [c_F, r_pr])], False)
-    r_pg = collect(T.p3, 16, [(T.FW, T.geo, False, []), (T.F, T.prod, False, [])])
-    c_gc = ev(V.tensor_copy(T.gcol[:, 0:1], T.gi[:, 0:1]))
-    c_m0 = ev(V.tensor_scalar(T.m0[:, 0:1], T.oi[:, 0:1], 0.0, None, A.is_equal))
-    c_i = ev(V.tensor_copy(T.icol[:, 0:1], T.oi[:, 0:1]))
-    wait("v", k_ps)
-    k_lo = ev(V.tensor_tensor(T.klo[:], T.kidc[:], T.p7[:, 0:384], A.subtract))
-    wait("v", i_qg, c_gc)
-    c_B = ev(V.tensor_scalar(T.Ball[:], T.qg[:], T.gcol[:, 0:1], None, A.is_equal))
-    wait("v", r_ps)
-    r_pos = ev(V.tensor_scalar(T.posS[:], T.p2[:, 0:16], -1.0, None, A.add))
-    wait("v", r_pos, fx)
-    r_sc = ev(V.tensor_copy(T.xq[:, 240:560].indirect(T.posS[:, 0:16]), T.x[:]))
-
-    c_m2 = ev(V.tensor_scalar(T.m2c[:, 0:1], T.oi[:, 0:1], 2.0, None, A.is_lt))
-    c_mB = ev(V.tensor_scalar(T.mB[:, 0:1], T.oi[:, 0:1], 14.0, None, A.is_ge))
-    wait("s", c_B, c_m0)
-    c_R0 = ev(S.activation(T.R0[:], T.Ball[:], AF.Identity, scale=T.m0[:, 0:1]))
-    wait("s", c_m2)
-    c_mb = ev(S.activation(T.m2b[:, 0:1], T.m2c[:, 0:1], AF.Copy))
-    wait("s", c_mB)
-    c_BB = ev(S.activation(T.BallB[:], T.Ball[:], AF.Identity, scale=T.mB[:, 0:1]))
-    c_FK = ev(S.activation(T.FK[:], T.F[:], AF.Identity, scale=T.m2c[:, 0:1]))
-    c_FB = ev(S.activation(T.FB[:], T.F[:], AF.Identity, scale=T.mB[:, 0:1]))
-    c_I16 = ev(S.activation(T.Id16[:], T.Id[:], AF.Copy, scale=16.0))
 
     near = [r for r in range(N) if r != own and topo.die(T.cores[r]) == topo.die(core)]
     far = [r for r in range(N) if r != own and topo.die(T.cores[r]) != topo.die(core)]
@@ -216,58 +121,185 @@ def rank_program(g, core, T, topo):
     for k, r in enumerate(near):
         masks[r] = topo.engines(core, T.cores[r])[1::2][4 * k:4 * k + 4]
 
-    def send(buf, sb, db, sem, lsem):
+    def send(src, sb, dst, db, n, sem):
         tr = []
         for r in far + near:
             rid, pid, _s = topo.addr(T.cores[r])
             a, b = sb(r), db(r)
             tr.append(RemoteDMATransfer(dst_ids=[DstId(rid=rid, pnc=pid)], dma_engine_mask=sum(1 << e for e in masks[r]),
-                                        remote_sem=sem, src=buf[:, a:a + CAP], dst=buf[:, b:b + CAP]))
-        g.remote_dma_fused(tr, local_sem=lsem)
+                                        remote_sem=T.sem[sem], src=src[:, a:a + n], dst=dst[:, b:b + n]))
+        g.remote_dma_fused(tr, local_sem=T.sem.left)
+        return (sem, 12)
 
+    def place(r):
+        return (own - r) % N - 1
+
+    Y.dma_start(T.spli[0:8, 0:4], T.spl[:]).then_inc(T.sem.sl, 16)
+    e_rt = dm(S.dma_start(T.roots[:, 4 * own:4 * own + 4], T.nk[:, 0:4]))
+    Y.dma_start(T.spli[0:8, 4:8], T.beg[:, 0:4]).then_inc(T.sem.sl, 16)
+    Y.dma_start(T.qq[0:112, 16:32], T.q[16:128, :]).then_inc(T.sem.ql, 16)
+    S.dma_start(T.qq[:, 0:16], T.q[:]).then_inc(T.sem.ql, 16)
+    Y.dma_start(T.qq[112:128, 16:32], T.q[0:16, :]).then_inc(T.sem.ql, 16)
+    e_beg = dm(S.dma_start(T.begc[:], T.beg[:]))
+    e_kid = dm(S.dma_start(T.kidc[:], T.kid[:]))
+    e_q, e_spl = ("ql", 48), ("sl", 32)
+    for o in range(16):
+        q = S if o < 7 else Y
+        q.dma_start(T.x[o::16, :], T.q[:]).then_inc(T.sem.xl, 16)
+    e_x = ("xl", 256)
+    f5 = dm(Y.dma_start(T.TB[:, ZC:6144], T.vec[:, 0:6144 - ZC]))
+    e_nk = [dm(Y.dma_start(T.nks[:, 0:NKA], T.nk[:, 0:NKA]))]
+
+    z = ev(V.memset(T.Z[:], 0.0))
+    f1 = ev(V.memset(T.TB[:, 0:ZA], 0.0))
+    k1 = ev(V.memset(T.keep[:], 16.0))
+    c_g0 = ev(V.memset(T.G[:, 0:16], 1.0))
+    c_g4 = ev(V.memset(T.G[:, 64:80], 0.0))
+    wait("v", k1)
+    c_kp = ev(V.memset(T.keep[:, 0:80:16], 0.0))
+    c_5 = ev(V.memset(T.five[:, 0:48], CAP / 16.0))
+    c_z = ev(V.memset(T.FF[:], 0.0))
+    f2 = ev(V.memset(T.TB[:, ZA:ZB], 0.0))
+    wait("g", z)
+    c_sel = ev(g.affine_select(T.sel[0:8, :], T.Z[0:8, 0:128], [[-1, 8], [0, 16]], A.not_equal, 1.0, 0, 1))
+    wait("p", c_sel)
+    p_B = ev(P.matmul(T.p1[:, 0:128], T.sel[0:8, :], T.sel[0:8, :], True, True))
+    wait("s", p_B)
+    c_B = ev(S.activation(T.Ball[:], T.p1[:, 0:128], AF.Copy))
+    c_nB = ev(S.activation(T.nBall[:], T.p1[:, 0:128], AF.Copy, scale=-1.0))
+    fx = ev(g.iota(T.W[:], [[0, NS]], FILL, 0))
+    wait("g", c_B)
+    c_U = ev(g.affine_select(T.U[:], T.Ball[:], [[-1, 128]], A.is_gt, 0.0, 0, 1))
+    c_Id = ev(g.affine_select(T.Id[:], T.Z[:, 0:128], [[-1, 128]], A.not_equal, 1.0, 0, 1))
+    wait("s", f1)
+    f0 = ev(S.activation(T.TB[:, ZB:ZB + 256], T.TB[:, 0:256], AF.Copy))
+    wait("s", c_U)
+    c_nU = ev(S.activation(T.nU[:], T.U[:], AF.Copy, scale=-1.0))
+    f3 = ev(S.activation(T.TB[:, ZB + 256:ZB + ZA], T.TB[:, 256:ZA], AF.Copy))
+    f4 = ev(S.activation(T.TB[:, ZB + ZA:ZC], T.TB[:, 0:ZA], AF.Copy))
+
+    wait("g", e_rt)
+    a_r = send(T.roots, lambda r: 4 * own, T.roots, lambda r: 4 * own, 4, "arrr")
+
+    wait("v", e_spl)
+    c_sf = ev(V.tensor_copy(T.splf[0:8, :], T.spli[0:8, :]))
+    wait("p", c_sf)
+    p_thr = ev(P.matmul(T.p0[:, 0:4], T.sel[0:8, :], T.splf[0:8, 0:4], True, True))
+    wait("v", e_beg)
+    b_hi = ev(V.tensor_copy(T.bhi[:], T.begc[:]))
+    wait("p", c_Id, b_hi)
+    b_ps = ev(P.matmul(T.p6[:, 0:192], T.Id[:], T.bhi[:], True, True))
+    wait("v", e_q)
+    r_t = ev(V.transpose(T.qt[:], T.qq[:]))
+    wait("v", e_kid)
+    k_hi = ev(V.tensor_copy(T.khi[:], T.kidc[:]))
+    wait("p", k_hi)
+    k_ps = ev(P.matmul(T.p7[:, 0:384], T.Id[:], T.khi[:], True, True))
+    wait("v", r_t, p_thr)
+    r_ge = together([V.tensor_scalar(T.G[:, 16 * o:16 * o + 16], T.qt[:, 0:16], T.p0[:, o:o + 1], None, A.is_ge)
+                     for o in (1, 2, 3)])
+    wait("v", c_kp, c_g0, c_g4, r_ge)
+    r_h = ev(V.tensor_tensor_scan(T.H[:], T.keep[:], T.G[:], 0.0, A.min, A.add))
+    PA, PB = T.p2[:, 0:48], T.p3[:, 0:16]
+    wait("p", c_B, c_5, c_nU, c_g0)
+    P.matmul(PA, T.Ball[:], T.five[:, 0:48], True, False)
+    P.matmul(PB, T.nU[:], T.G[:, 0:16], True, False)
+    d0 = ev(P.matmul(T.p4[:, 0:1], T.nU[:], T.G[:, 0:1], True, True))
+    wait("p", c_U, c_g4, r_ge)
+    for m, a in ((T.nU, 16), (T.nU, 16), (T.U, 0), (T.U, 32)):
+        P.matmul(PA, m[:], T.G[:, a:a + 48], False, False)
+    P.matmul(PB, T.U[:], T.G[:, 16:32], False, False)
+    wait("p", c_nB, r_h)
+    for m, a in ((T.Ball, 16), (T.Ball, 16), (T.nBall, 0)):
+        P.matmul(PA, m[:], T.H[:, a:a + 48], False, False)
+    r_d = ev(P.matmul(PA, T.nBall[:], T.H[:, 32:80], False, True))
+    P.matmul(PB, T.Ball[:], T.H[:, 0:16], False, False)
+    P.matmul(PB, T.nBall[:], T.H[:, 16:32], False, False)
+    wait("v", k_ps)
+    k_lo = ev(V.tensor_tensor(T.klo[:], T.kidc[:], T.p7[:, 0:384], A.subtract))
+    wait("v", r_d)
+    r_pr = ev(V.tensor_tensor(T.prod[:, 0:48], PA, T.G[:, 16:64], A.mult))
+    wait("p", r_pr)
+    P.matmul(PB, T.Id[:], T.prod[:, 0:16], False, False)
+    P.matmul(PB, T.Id[:], T.prod[:, 16:32], False, False)
+    r_ps = ev(P.matmul(PB, T.Id[:], T.prod[:, 32:48], False, True))
+    wait("v", b_ps)
+    b_lo = ev(V.tensor_tensor(T.blo[:], T.begc[:], T.p6[:, 0:192], A.subtract))
+    wait("v", r_ps)
+    r_pos = ev(V.tensor_scalar(T.posS[:], PB, -1.0, None, A.add))
+    wait("v", r_pos, fx, e_x)
+    r_sc = ev(V.tensor_copy(T.W[:].indirect(T.posS[:]), T.x[:]))
     wait("g", r_sc)
-    send(T.xq, lambda r: 240 + CAP * ((r - own) % N), lambda r: CAP * ((own - r) % N - 1), T.sem.arrx, T.sem.lsx)
-    a_x = ("arrx", 12)
+    a_x = send(T.W, lambda r: CAP * r, T.X, lambda r: CAP * place(r), CAP, "arrx")
     g.sem_inc(T.sem.sent, 1)
 
-    wait("y", b_hi, b_lo, f1, f3, f4, *f2)
+    P.matmul(T.p0[:, 4:5], T.sel[0:8, :], T.splf[0:8, 4:5], True, False)
+    d00 = ev(P.matmul(T.p0[:, 4:5], T.nU[:], T.G[:, 0:1], False, True))
+    wait("s", d0, c_z)
+    m0 = ev(S.activation(T.mt[:, 0:1], T.p4[:, 0:1], AF.Relu, bias=-13.0, scale=-1.0))
+    m1 = ev(S.activation(T.mt[:, 1:2], T.p4[:, 0:1], AF.Relu, bias=2.0))
+    c_F = ev(S.activation(T.FF[:, F + 16:F + 144:16], T.Ball[:, 0:128:16], AF.Copy))
+    wait("s", m0, m1)
+    m2 = ev(S.activation(T.mf[:, 0:2], T.mt[:, 0:2], AF.Sign))
+    c_mK = ev(S.activation(T.mK[:, 0:1], T.mt[:, 0:1], AF.Sign))
+    wait("s", m2)
+    c_FK = ev(S.activation(T.FF[:, FK + 16:FK + 144:16], T.Ball[:, 0:128:16], AF.Identity, scale=T.mf[:, 0:1]))
+    c_FB = ev(S.activation(T.FF[:, FB + 16:FB + 144:16], T.Ball[:, 0:128:16], AF.Identity, scale=T.mf[:, 1:2]))
+    wait("s", r_pos)
+    g_c = ev(S.activation(T.pg[:, 0:16], PB, AF.Identity, bias=-1.0))
+
+    wait("y", b_hi, k_hi, f0, f1, f2, f3, f4, f5)
     t_b = dm(Y.dma_start(T.TB[14::16, 0:3072], T.bhi[:]))
-    t_c = dm(Y.dma_start(T.TB[15::16, 0:3072], T.blo[:]))
-    wait("y", k_hi, k_lo)
     t_k = dm(Y.dma_start(T.TB[0::16, :], T.khi[:]))
+    wait("y", k_lo)
     t_l = dm(Y.dma_start(T.TB[1::16, :], T.klo[:]))
+    wait("y", b_lo)
+    t_c = dm(Y.dma_start(T.TB[15::16, 0:3072], T.blo[:]))
     e_nk.append(dm(Y.dma_start(T.nks[:, NKA:NKB], T.nk[:, NKA:NKB])))
-    wait("y", ("sent", 1))
+    wait("y", ("sent", 1), g_c)
     e_nk.append(dm(Y.dma_start(T.nks[:, NKB:3072], T.nk[:, NKB:3072])))
-    e_vec = dm(Y.dma_start(T.vecs[:], T.vec[:]))
+    Y.dma_start(T.pg[0:112, 16:32], T.pg[16:128, 0:16]).then_inc(T.sem.pl, 16)
+    Y.dma_start(T.pg[112:128, 16:32], T.pg[0:16, 0:16]).then_inc(T.sem.pl, 16)
     tb = [t_k, t_l, t_b, t_c]
 
-    X = T.xq[:, 0:NS]
-    wait("p", c_R0, b_hi, b_lo)
-    P.matmul(T.p4[:, 0:1], T.R0[:], T.bhi[:, 0:1], True, False)
-    d0 = ev(P.matmul(T.p4[:, 0:1], T.R0[:], T.blo[:, 0:1], False, True))
-    wait("v", d0, c_i)
-    d1 = ev(V.tensor_scalar(T.e1[:, 0:8], T.Z[:, 0:8], T.p4[:, 0:1], T.icol[:, 0:1], A.add, A.add))
-    wait("v", d1, *tb)
+    wait("v", e_rt, a_r)
+    c_rt = ev(V.tensor_copy(T.rootf[:], T.roots[:]))
+    wait("v", d00)
+    d1 = ev(V.tensor_scalar(T.e1[:, 0:8], T.Z[:, 0:8], T.p0[:, 4:5], 15.0, A.add, A.add))
+    wait("v", r_sc, c_rt)
+    w1 = together([V.tensor_scalar(T.ge1[:, CAP * r:CAP * r + CAP], T.W[:, CAP * r:CAP * r + CAP],
+                                   T.rootf[:, 4 * r:4 * r + 1], None, A.is_ge) for r in range(N)])
+    q1 = collect(T.p5, 20, F, T.ge1, [c_F, w1])
+    x_own = ev(V.tensor_copy(T.X[:, 240:320], T.W[:, CAP * own:CAP * own + CAP]))
+    wait("v", d1, c_B, *tb)
     d2 = ev(V.tensor_tensor(T.km[:], T.TB[:].indirect(T.e1[:, 0:8]), T.Ball[:], A.mult))
-    wait("p", c_mb, d2)
-    d3 = ev(P.matmul(T.p5[:, 0:1], T.km[:], T.m2b[:, 0:1], True, True))
-    wait("v", d3)
-    d4 = ev(V.tensor_copy(T.ml2[:, 0:1], T.p5[:, 0:1]))
-    wait("v", d4)
-    d5 = ev(V.tensor_copy(T.bm[:], T.TB[:, 0:3072].indirect(T.ml2[:, 0:1])))
-    wait("p", c_BB, d5)
-    d6 = ev(P.matmul(T.p6[:, 0:16], T.BallB[:], T.bm[:], True, True))
-    wait("v", r_pg)
-    r_posg = ev(V.tensor_scalar(T.posG[:], T.p3[:, 0:16], -1.0, None, A.add))
-    wait("v", e_nk[0])
-    c_rt = ev(V.tensor_copy(T.rootc[:, 0:1], T.nks[:, 0:1]))
+    wait("v", q1)
+    s2 = ev(V.tensor_scalar(T.s2[:], T.p5[:, 0:20], -1.0, None, A.add))
+    s2b = ev(V.tensor_scalar(T.s2b[:, 0:5], T.p5[:, 5 * own:5 * own + 5], -1.0, None, A.add))
+    wait("g", s2)
+    a_l = send(T.s2, lambda r: 5 * r, T.s2a, lambda r: 5 * place(r), 5, "arrl")
+    g.sem_inc(T.sem.sent, 1)
+    wait("y", ("sent", 2))
+    e_vec = dm(Y.dma_start(T.vecs[:], T.vec[:]))
 
-    def to_list(buf, ps, event, add):
-        wait("v", event)
-        e = ev(V.tensor_scalar(buf[:], ps[:, 0:20], float(add), None, A.add))
-        wait("v", e)
-        return e
+    wait("p", c_mK, d2)
+    d3 = ev(P.matmul(T.p7[:, 0:1], T.km[:], T.mK[:, 0:1], True, True))
+    P.matmul(T.p6[:, 0:16], T.nU[:], T.G[:, 0:16], True, False)
+    wait("v", d3)
+    d4 = ev(V.tensor_copy(T.ml2[:, 0:1], T.p7[:, 0:1]))
+    wait("v", d4, m2)
+    d5 = ev(V.tensor_scalar(T.bm[:], T.TB[:, 0:3072].indirect(T.ml2[:, 0:1]), T.mf[:, 1:2], None, A.mult))
+    wait("p", d5)
+    d6 = ev(P.matmul(T.p6[:, 0:16], T.Ball[:], T.bm[:], False, True))
+    wait("v", d6)
+    d7 = ev(V.tensor_scalar(T.e2[:], T.p6[:, 0:16], 15.0, None, A.add))
+    wait("s", d7, *tb)
+    d9 = ev(S.activation(T.kg3[:, 128:256], T.TB[:].indirect(T.e2[:, 8:16]), AF.Copy))
+    wait("v", d7)
+    d8 = ev(V.tensor_copy(T.kg3[:, 0:128], T.TB[:].indirect(T.e2[:, 0:8])))
+    d10 = collect(T.p4, 16, FK, T.kg3, [c_FK, d8, d9])
+    wait("v", *e_nk)
+    d11 = ev(V.tensor_copy(T.nk2[:], T.nks[:].indirect(T.ml2[:, 0:1])))
 
     def two_lists(buf, ps, event, add):
         wait("v", event)
@@ -278,12 +310,12 @@ def rank_program(g, core, T, topo):
         ea = ev(S.activation(bp[:, 64:160], starts.indirect(lst[:, 4:10]), AF.Copy))
         wait("v", el[0], *deps_v, *deps_s)
         eb = ev(V.tensor_copy(bp[:, 0:64], starts.indirect(lst[:, 0:4])))
-        g0 = ev(V.tensor_tensor(ge[:, 0:160], keys.indirect(lst[:, 0:10]), T.xq[:, 0:160], A.is_le))
+        g0 = ev(V.tensor_tensor(ge[:, 0:160], keys.indirect(lst[:, 0:10]), T.X[:, 0:160], A.is_le))
         wait("s", el[1])
         ec = ev(S.activation(bp[:, 160:320], starts.indirect(lst[:, 10:20]), AF.Copy))
         wait("v", el[1])
-        g1 = ev(V.tensor_tensor(ge[:, 160:320], keys.indirect(lst[:, 10:20]), T.xq[:, 160:320], A.is_le))
-        return halves(ps, [(T.FB, bp, 0, [c_FB, ea, eb]), (T.F, ge, 0, [g0]), (T.FB, bp, 1, [ec]), (T.F, ge, 1, [g1])])
+        g1 = ev(V.tensor_tensor(ge[:, 160:320], keys.indirect(lst[:, 10:20]), T.X[:, 160:320], A.is_le))
+        return halves(ps, [(FB, bp, 0, [c_FB, ea, eb]), (F, ge, 0, [g0]), (FB, bp, 1, [ec]), (F, ge, 1, [g1])])
 
     def child(lst, el, kg, ps):
         ee = []
@@ -294,37 +326,25 @@ def rank_program(g, core, T, topo):
             wait("v", el[h])
             b = ev(V.tensor_copy(kg[:, 16 * c:16 * (c + va)], T.TB[:].indirect(lst[:, c:c + va])))
             ee.append([a, b])
-        return halves(ps, [(T.FK, kg, 0, [c_FK] + ee[0]), (T.FK, kg, 1, ee[1])])
+        return halves(ps, [(FK, kg, 0, [c_FK] + ee[0]), (FK, kg, 1, ee[1])])
 
-    wait("v", r_sc, c_rt)
-    w0 = ev(V.tensor_scalar(T.ge1[:, 240:320], T.xq[:, 240:320], T.rootc[:, 0:1], None, A.is_ge))
-    wait("v", a_x)
-    w1 = ev(V.tensor_scalar(T.ge1[:, 0:240], T.xq[:, 0:240], T.rootc[:, 0:1], None, A.is_ge))
-    q1 = collect(T.p5, 20, [(T.F, T.ge1, True, [c_F, w0, w1])])
-    wait("v", d6)
-    d7 = ev(V.tensor_scalar(T.e2[:], T.p6[:, 0:16], T.icol[:, 0:1], None, A.add))
-    wait("v", d7)
-    d8 = ev(V.tensor_copy(T.kg3[:, 0:128], T.TB[:].indirect(T.e2[:, 0:8])))
-    wait("s", d7, *tb)
-    d9 = ev(S.activation(T.kg3[:, 128:256], T.TB[:].indirect(T.e2[:, 8:16]), AF.Copy))
-    d10 = collect(T.p4, 16, [(T.FK, T.kg3, True, [c_FK, d8, d9])])
-    wait("v", *e_nk)
-    d11 = ev(V.tensor_copy(T.nk2[:], T.nks[:].indirect(T.ml2[:, 0:1])))
-    s2 = to_list(T.s2, T.p5, q1, -1)
-    wait("s", s2)
-    s2f = ev(S.activation(T.s2f[:], T.p5[:, 0:20], AF.Copy))
-    wait("v", d11)
-    w2 = ev(V.tensor_tensor(T.ge2[:], T.nk2[:].indirect(T.s2[:]), X, A.is_le))
-    wait("p", s2f, c_I16)
-    P.matmul(T.p6[:, 0:20], T.Id16[:], T.s2f[:], True, False)
-    q2 = collect(T.p6, 20, [(T.F, T.ge2, True, [w2])], False)
+    wait("v", d11, x_own, s2b)
+    w2 = [ev(V.tensor_tensor(T.ge2[:, 240:320], T.nk2[:].indirect(T.s2b[:, 0:5]), T.X[:, 240:320], A.is_le))]
+    wait("v", a_x, a_l)
+    w2.append(ev(V.tensor_tensor(T.ge2[:, 0:240], T.nk2[:].indirect(T.s2a[:, 0:15]), T.X[:, 0:240], A.is_le)))
+    s2f = together([V.tensor_scalar(T.s2f[:, 0:15], T.s2a[:, 0:15], 16.0, None, A.mult),
+                    V.tensor_scalar(T.s2f[:, 15:20], T.s2b[:, 0:5], 16.0, None, A.mult)])
+    collect(T.p6, 20, F, T.ge2, w2 + [d7, s2], False)
+    wait("p", s2f)
+    q2 = ev(P.matmul(T.p6[:, 0:20], T.Id[:], T.s2f[:, 0:20], False, True))
     wait("v", d10)
     d12 = ev(V.tensor_copy(T.ml3[:], T.p4[:, 0:16]))
     wait("s", d12)
     d14 = ev(S.activation(T.bl3[:], T.TB[:, 0:3072].indirect(T.ml3[:]), AF.Copy))
     wait("v", d12)
     d13 = ev(V.tensor_copy(T.nk3[:], T.nks[:].indirect(T.ml3[:])))
-    s3 = to_list(T.s3, T.p6, q2, -17)
+    wait("v", q2)
+    s3 = ev(V.tensor_scalar(T.s3[:], T.p6[:, 0:20], -1.0, None, A.add))
     e3 = two_lists(T.e3, T.p4, level(T.nk3[:], T.bl3[:], T.s3, [s3, s3], T.ge3, T.bp3, T.p4, [d13], [d14]), -1)
     n4 = two_lists(T.n4, T.p5, child(T.e3, e3, T.kg4, T.p5), 0)
     e4 = two_lists(T.e4, T.p6, level(T.nks[:], T.TB[:, 0:3072], T.n4, n4, T.ge4, T.bp4, T.p6, [], []), -1)
@@ -333,20 +353,25 @@ def rank_program(g, core, T, topo):
     vl = two_lists(T.vl, T.p6, child(T.e5, e5, T.kg6, T.p6), 0)
 
     wait("v", e_vec, vl[0])
-    va = ev(V.tensor_copy(T.ansb[:, 0:128], T.vecs[:].indirect(T.vl[:, 0:8])))
+    va = ev(V.tensor_copy(T.An[:, 0:128], T.vecs[:].indirect(T.vl[:, 0:8])))
     wait("s", e_vec, *vl)
-    vb = ev(S.activation(T.ansb[:, 128:256], T.vecs[:].indirect(T.vl[:, 8:16]), AF.Copy))
+    vb = ev(S.activation(T.An[:, 128:256], T.vecs[:].indirect(T.vl[:, 8:16]), AF.Copy))
     wait("v", vl[1])
-    vc = ev(V.tensor_copy(T.ansb[:, 256:320], T.vecs[:].indirect(T.vl[:, 16:20])))
+    vc = ev(V.tensor_copy(T.An[:, 256:320], T.vecs[:].indirect(T.vl[:, 16:20])))
     wait("g", va, vb)
-    send(T.ansb, lambda r: CAP * ((r - own) % N - 1), lambda r: 240 + CAP * ((own - r) % N), T.sem.arry, T.sem.lsy)
-    a_y = ("arry", 12)
+    a_y = send(T.An, lambda r: CAP * ((r - own) % N - 1), T.R, lambda r: CAP * own, CAP, "arry")
 
-    wait("v", a_y, va, vb, vc, r_posg)
-    wait("s", a_y, va, vb, vc, r_posg)
-    y1 = ev(V.tensor_copy(T.yb[:, 0:128], T.ansb[:, 240:560].indirect(T.posG[:, 0:8])))
-    y2 = ev(S.activation(T.yb[:, 128:256], T.ansb[:, 240:560].indirect(T.posG[:, 8:16]), AF.Copy))
+    wait("v", ("pl", 32))
+    g_t = ev(V.transpose(T.pt[:], T.pg[:]))
+    wait("v", vb, vc)
+    y0 = ev(V.tensor_copy(T.R[:, CAP * own:CAP * own + CAP], T.An[:, 240:320]))
+    wait("v", g_t)
+    r_posg = ev(V.tensor_copy(T.posG[:], T.pt[:, 0:16]))
+    wait("v", a_y, y0, r_posg)
+    wait("s", a_y, y0, r_posg)
+    y1 = ev(V.tensor_copy(T.yb[:, 0:128], T.R[:].indirect(T.posG[:, 0:8])))
+    y2 = ev(S.activation(T.yb[:, 128:256], T.R[:].indirect(T.posG[:, 8:16]), AF.Copy))
     wait("y", y1, y2)
     st = dm(Y.dma_start(T.y[:], T.yb[:]))
     wait("y", st)
-    wait("g", ("lsx", 12), ("lsy", 12))
+    wait("g", ("left", 48))

from concourse.bass import DstId, RemoteDMATransfer
from concourse.mybir import AluOpType as A, ActivationFunctionType as AF

CAP = 80
NS = 4 * CAP
FILL = 16777214
NKA, NKB = 1536, 2304
ZA, ZB, ZC = 1088, 2432, 4608

SCRATCH = {
    "x": ("sbuf", [128, 256], "int32"),
    "W": ("sbuf", [128, NS], "int32"),
    "X": ("sbuf", [128, NS], "int32"),
    "An": ("sbuf", [128, NS], "bfloat16"),
    "R": ("sbuf", [128, NS], "bfloat16"),
    "yb": ("sbuf", [128, 256], "bfloat16"),
    "nks": ("sbuf", [128, 3072], "int32"),
    "vecs": ("sbuf", [128, 3072], "bfloat16"),
    "TB": ("sbuf", [128, 6144], "bfloat16"),
    "kidc": ("sbuf", [128, 384], "int32"),
    "begc": ("sbuf", [128, 192], "int32"),
    "khi": ("sbuf", [128, 384], "bfloat16"),
    "klo": ("sbuf", [128, 384], "bfloat16"),
    "bhi": ("sbuf", [128, 192], "bfloat16"),
    "blo": ("sbuf", [128, 192], "bfloat16"),
    "Z": ("sbuf", [128, 160], "bfloat16"),
    "qq": ("sbuf", [128, 32], "int32"),
    "qt": ("sbuf", [128, 32], "int32"),
    "pg": ("sbuf", [128, 32], "float32"),
    "pt": ("sbuf", [128, 32], "float32"),
    "spli": ("sbuf", [128, 8], "int32"),
    "splf": ("sbuf", [128, 8], "float32"),
    "roots": ("sbuf", [128, 16], "int32"),
    "rootf": ("sbuf", [128, 16], "float32"),
    "mt": ("sbuf", [128, 8], "float32"),
    "mf": ("sbuf", [128, 8], "float32"),
    "mK": ("sbuf", [128, 16], "bfloat16"),
    "FF": ("sbuf", [128, 432], "bfloat16"),
    "sel": ("sbuf", [128, 128], "float32"),
    "s2f": ("sbuf", [128, 32], "bfloat16"),
    "bm": ("sbuf", [128, 16], "bfloat16"),
    "nk2": ("sbuf", [128, 16], "int32"),
    "nk3": ("sbuf", [128, 256], "int32"),
}
for _n in ("G", "H", "keep", "five", "prod"):
    SCRATCH[_n] = ("sbuf", [128, 80], "bfloat16")
for _n in ("Id", "Ball", "nBall", "U", "nU", "km"):
    SCRATCH[_n] = ("sbuf", [128, 128], "bfloat16")
for _n in ("kg3", "bl3"):
    SCRATCH[_n] = ("sbuf", [128, 256], "bfloat16")
for _n in ("posS", "posG", "e1", "ml2", "e2", "ml3", "s2a", "s2b"):
    SCRATCH[_n] = ("sbuf", [128, 16], "uint16")
for _n in ("s2", "s3", "e3", "n4", "e4", "n5", "e5", "vl"):
    SCRATCH[_n] = ("sbuf", [128, 20], "uint16")
for _n in ("ge1", "ge2", "ge3", "ge4", "ge5", "kg4", "kg5", "kg6", "bp3", "bp4", "bp5"):
    SCRATCH[_n] = ("sbuf", [128, NS], "bfloat16")
for _n in range(8):
    SCRATCH["p%d" % _n] = ("psum", [128, 512], "float32")

SEMAPHORES = ["arrr", "arrx", "arrl", "arry", "left", "xl", "ql", "sl", "pl", "sent"] + ["e%d" % _k for _k in range(140)]


def rank_program(g, core, T, topo):
    own = T.rank_of(core)
    if own is None:
        return
    N = 4
    V, S, P, Y = g.vector, g.scalar, g.tensor, g.sync
    F, FK, FB = 0, 144, 288
    used = [0]
    done = {"v": {}, "s": {}, "p": {}, "y": {}, "g": {}}
    names = (("v", V), ("s", S), ("p", P), ("y", Y), ("g", g))

    def ev(inst, n=1):
        k = "e%d" % used[0]
        used[0] += 1
        inst.then_inc(T.sem[k], n)
        return (k, n)

    def together(insts):
        k, _n = ev(insts[0])
        for inst in insts[1:]:
            inst.then_inc(T.sem[k], 1)
        return (k, len(insts))

    def dm(inst):
        return ev(inst, 16)

    def wait(q, *events):
        for name, queue in names:
            if name == q:
                for k, n in events:
                    if done[q].get(k, 0) < n:
                        queue.wait_ge(T.sem[k], n)
                        done[q][k] = n

    def collect(ps, n, fb, rhs, events, close=True):
        wait("p", *events)
        last = None
        for i in range(16):
            last = P.matmul(ps[:, 0:n], T.FF[:, fb + 16 - i:fb + 144 - i], rhs[:, i:16 * n:16], i == 0, close and i == 15)
        return ev(last) if close else None

    def halves(ps, terms):
        tot = 8 * len(terms)
        k = 0
        last = None
        for fb, rhs, h, events in terms:
            wait("p", *events)
            for i in range(8):
                a = fb + 16 - 8 * h - i
                last = P.matmul(ps[:, 0:20], T.FF[:, a:a + 128], rhs[:, 160 * h + i:160 * h + 160:8], k == 0, k == tot - 1)
                k += 1
        return ev(last)

    near = [r for r in range(N) if r != own and topo.die(T.cores[r]) == topo.die(core)]
    far = [r for r in range(N) if r != own and topo.die(T.cores[r]) != topo.die(core)]
    masks = {}
    for k, r in enumerate(far):
        masks[r] = topo.engines(core, T.cores[r])[0::2][4 * k:4 * k + 4]
    for k, r in enumerate(near):
        masks[r] = topo.engines(core, T.cores[r])[1::2][4 * k:4 * k + 4]

    def send(src, sb, dst, db, n, sem):
        tr = []
        for r in far + near:
            rid, pid, _s = topo.addr(T.cores[r])
            a, b = sb(r), db(r)
            tr.append(RemoteDMATransfer(dst_ids=[DstId(rid=rid, pnc=pid)], dma_engine_mask=sum(1 << e for e in masks[r]),
                                        remote_sem=T.sem[sem], src=src[:, a:a + n], dst=dst[:, b:b + n]))
        g.remote_dma_fused(tr, local_sem=T.sem.left)
        return (sem, 12)

    def place(r):
        return (own - r) % N - 1

    Y.dma_start(T.spli[0:8, 0:4], T.spl[:]).then_inc(T.sem.sl, 16)
    e_rt = dm(S.dma_start(T.roots[:, 4 * own:4 * own + 4], T.nk[:, 0:4]))
    Y.dma_start(T.spli[0:8, 4:8], T.beg[:, 0:4]).then_inc(T.sem.sl, 16)
    Y.dma_start(T.qq[0:112, 16:32], T.q[16:128, :]).then_inc(T.sem.ql, 16)
    S.dma_start(T.qq[:, 0:16], T.q[:]).then_inc(T.sem.ql, 16)
    Y.dma_start(T.qq[112:128, 16:32], T.q[0:16, :]).then_inc(T.sem.ql, 16)
    e_beg = dm(S.dma_start(T.begc[:], T.beg[:]))
    e_kid = dm(S.dma_start(T.kidc[:], T.kid[:]))
    e_q, e_spl = ("ql", 48), ("sl", 32)
    for o in range(16):
        q = S if o < 7 else Y
        q.dma_start(T.x[o::16, :], T.q[:]).then_inc(T.sem.xl, 16)
    e_x = ("xl", 256)
    f5 = dm(Y.dma_start(T.TB[:, ZC:6144], T.vec[:, 0:6144 - ZC]))
    e_nk = [dm(Y.dma_start(T.nks[:, 0:NKA], T.nk[:, 0:NKA]))]

    z = ev(V.memset(T.Z[:], 0.0))
    f1 = ev(V.memset(T.TB[:, 0:ZA], 0.0))
    k1 = ev(V.memset(T.keep[:], 16.0))
    c_g0 = ev(V.memset(T.G[:, 0:16], 1.0))
    c_g4 = ev(V.memset(T.G[:, 64:80], 0.0))
    wait("v", k1)
    c_kp = ev(V.memset(T.keep[:, 0:80:16], 0.0))
    c_5 = ev(V.memset(T.five[:, 0:48], CAP / 16.0))
    c_z = ev(V.memset(T.FF[:], 0.0))
    f2 = ev(V.memset(T.TB[:, ZA:ZB], 0.0))
    wait("g", z)
    c_sel = ev(g.affine_select(T.sel[0:8, :], T.Z[0:8, 0:128], [[-1, 8], [0, 16]], A.not_equal, 1.0, 0, 1))
    wait("p", c_sel)
    p_B = ev(P.matmul(T.p1[:, 0:128], T.sel[0:8, :], T.sel[0:8, :], True, True))
    wait("s", p_B)
    c_B = ev(S.activation(T.Ball[:], T.p1[:, 0:128], AF.Copy))
    c_nB = ev(S.activation(T.nBall[:], T.p1[:, 0:128], AF.Copy, scale=-1.0))
    fx = ev(g.iota(T.W[:], [[0, NS]], FILL, 0))
    wait("g", c_B)
    c_U = ev(g.affine_select(T.U[:], T.Ball[:], [[-1, 128]], A.is_gt, 0.0, 0, 1))
    c_Id = ev(g.affine_select(T.Id[:], T.Z[:, 0:128], [[-1, 128]], A.not_equal, 1.0, 0, 1))
    wait("s", f1)
    f0 = ev(S.activation(T.TB[:, ZB:ZB + 256], T.TB[:, 0:256], AF.Copy))
    wait("s", c_U)
    c_nU = ev(S.activation(T.nU[:], T.U[:], AF.Copy, scale=-1.0))
    f3 = ev(S.activation(T.TB[:, ZB + 256:ZB + ZA], T.TB[:, 256:ZA], AF.Copy))
    f4 = ev(S.activation(T.TB[:, ZB + ZA:ZC], T.TB[:, 0:ZA], AF.Copy))

    wait("g", e_rt)
    a_r = send(T.roots, lambda r: 4 * own, T.roots, lambda r: 4 * own, 4, "arrr")

    wait("v", e_spl)
    c_sf = ev(V.tensor_copy(T.splf[0:8, :], T.spli[0:8, :]))
    wait("p", c_sf)
    p_thr = ev(P.matmul(T.p0[:, 0:4], T.sel[0:8, :], T.splf[0:8, 0:4], True, True))
    wait("v", e_beg)
    b_hi = ev(V.tensor_copy(T.bhi[:], T.begc[:]))
    wait("p", c_Id, b_hi)
    b_ps = ev(P.matmul(T.p6[:, 0:192], T.Id[:], T.bhi[:], True, True))
    wait("v", e_q)
    r_t = ev(V.transpose(T.qt[:], T.qq[:]))
    wait("v", e_kid)
    k_hi = ev(V.tensor_copy(T.khi[:], T.kidc[:]))
    wait("p", k_hi)
    k_ps = ev(P.matmul(T.p7[:, 0:384], T.Id[:], T.khi[:], True, True))
    wait("v", r_t, p_thr)
    r_ge = together([V.tensor_scalar(T.G[:, 16 * o:16 * o + 16], T.qt[:, 0:16], T.p0[:, o:o + 1], None, A.is_ge)
                     for o in (1, 2, 3)])
    wait("v", c_kp, c_g0, c_g4, r_ge)
    r_h = ev(V.tensor_tensor_scan(T.H[:], T.keep[:], T.G[:], 0.0, A.min, A.add))
    PA, PB = T.p2[:, 0:48], T.p3[:, 0:16]
    wait("p", c_B, c_5, c_nU, c_g0)
    P.matmul(PA, T.Ball[:], T.five[:, 0:48], True, False)
    P.matmul(PB, T.nU[:], T.G[:, 0:16], True, False)
    d0 = ev(P.matmul(T.p4[:, 0:1], T.nU[:], T.G[:, 0:1], True, True))
    wait("p", c_U, c_g4, r_ge)
    for m, a in ((T.nU, 16), (T.nU, 16), (T.U, 0), (T.U, 32)):
        P.matmul(PA, m[:], T.G[:, a:a + 48], False, False)
    P.matmul(PB, T.U[:], T.G[:, 16:32], False, False)
    wait("p", c_nB, r_h)
    for m, a in ((T.Ball, 16), (T.Ball, 16), (T.nBall, 0)):
        P.matmul(PA, m[:], T.H[:, a:a + 48], False, False)
    r_d = ev(P.matmul(PA, T.nBall[:], T.H[:, 32:80], False, True))
    P.matmul(PB, T.Ball[:], T.H[:, 0:16], False, False)
    P.matmul(PB, T.nBall[:], T.H[:, 16:32], False, False)
    wait("v", k_ps)
    k_lo = ev(V.tensor_tensor(T.klo[:], T.kidc[:], T.p7[:, 0:384], A.subtract))
    wait("v", r_d)
    r_pr = ev(V.tensor_tensor(T.prod[:, 0:48], PA, T.G[:, 16:64], A.mult))
    wait("p", r_pr)
    P.matmul(PB, T.Id[:], T.prod[:, 0:16], False, False)
    P.matmul(PB, T.Id[:], T.prod[:, 16:32], False, False)
    r_ps = ev(P.matmul(PB, T.Id[:], T.prod[:, 32:48], False, True))
    wait("v", b_ps)
    b_lo = ev(V.tensor_tensor(T.blo[:], T.begc[:], T.p6[:, 0:192], A.subtract))
    wait("v", r_ps)
    r_pos = ev(V.tensor_scalar(T.posS[:], PB, -1.0, None, A.add))
    wait("v", r_pos, fx, e_x)
    r_sc = ev(V.tensor_copy(T.W[:].indirect(T.posS[:]), T.x[:]))
    wait("g", r_sc)
    a_x = send(T.W, lambda r: CAP * r, T.X, lambda r: CAP * place(r), CAP, "arrx")
    g.sem_inc(T.sem.sent, 1)

    P.matmul(T.p0[:, 4:5], T.sel[0:8, :], T.splf[0:8, 4:5], True, False)
    d00 = ev(P.matmul(T.p0[:, 4:5], T.nU[:], T.G[:, 0:1], False, True))
    wait("s", d0, c_z)
    m0 = ev(S.activation(T.mt[:, 0:1], T.p4[:, 0:1], AF.Relu, bias=-13.0, scale=-1.0))
    m1 = ev(S.activation(T.mt[:, 1:2], T.p4[:, 0:1], AF.Relu, bias=2.0))
    c_F = ev(S.activation(T.FF[:, F + 16:F + 144:16], T.Ball[:, 0:128:16], AF.Copy))
    wait("s", m0, m1)
    m2 = ev(S.activation(T.mf[:, 0:2], T.mt[:, 0:2], AF.Sign))
    c_mK = ev(S.activation(T.mK[:, 0:1], T.mt[:, 0:1], AF.Sign))
    wait("s", m2)
    c_FK = ev(S.activation(T.FF[:, FK + 16:FK + 144:16], T.Ball[:, 0:128:16], AF.Identity, scale=T.mf[:, 0:1]))
    c_FB = ev(S.activation(T.FF[:, FB + 16:FB + 144:16], T.Ball[:, 0:128:16], AF.Identity, scale=T.mf[:, 1:2]))
    wait("s", r_pos)
    g_c = ev(S.activation(T.pg[:, 0:16], PB, AF.Identity, bias=-1.0))

    wait("y", b_hi, k_hi, f0, f1, f2, f3, f4, f5)
    t_b = dm(Y.dma_start(T.TB[14::16, 0:3072], T.bhi[:]))
    t_k = dm(Y.dma_start(T.TB[0::16, :], T.khi[:]))
    wait("y", k_lo)
    t_l = dm(Y.dma_start(T.TB[1::16, :], T.klo[:]))
    wait("y", b_lo)
    t_c = dm(Y.dma_start(T.TB[15::16, 0:3072], T.blo[:]))
    e_nk.append(dm(Y.dma_start(T.nks[:, NKA:NKB], T.nk[:, NKA:NKB])))
    wait("y", ("sent", 1), g_c)
    e_nk.append(dm(Y.dma_start(T.nks[:, NKB:3072], T.nk[:, NKB:3072])))
    Y.dma_start(T.pg[0:112, 16:32], T.pg[16:128, 0:16]).then_inc(T.sem.pl, 16)
    Y.dma_start(T.pg[112:128, 16:32], T.pg[0:16, 0:16]).then_inc(T.sem.pl, 16)
    tb = [t_k, t_l, t_b, t_c]

    wait("v", e_rt, a_r)
    c_rt = ev(V.tensor_copy(T.rootf[:], T.roots[:]))
    wait("v", d00)
    d1 = ev(V.tensor_scalar(T.e1[:, 0:8], T.Z[:, 0:8], T.p0[:, 4:5], 15.0, A.add, A.add))
    wait("v", r_sc, c_rt)
    w1 = together([V.tensor_scalar(T.ge1[:, CAP * r:CAP * r + CAP], T.W[:, CAP * r:CAP * r + CAP],
                                   T.rootf[:, 4 * r:4 * r + 1], None, A.is_ge) for r in range(N)])
    q1 = collect(T.p5, 20, F, T.ge1, [c_F, w1])
    x_own = ev(V.tensor_copy(T.X[:, 240:320], T.W[:, CAP * own:CAP * own + CAP]))
    wait("v", d1, c_B, *tb)
    d2 = ev(V.tensor_tensor(T.km[:], T.TB[:].indirect(T.e1[:, 0:8]), T.Ball[:], A.mult))
    wait("v", q1)
    s2 = ev(V.tensor_scalar(T.s2[:], T.p5[:, 0:20], -1.0, None, A.add))
    s2b = ev(V.tensor_scalar(T.s2b[:, 0:5], T.p5[:, 5 * own:5 * own + 5], -1.0, None, A.add))
    wait("g", s2)
    a_l = send(T.s2, lambda r: 5 * r, T.s2a, lambda r: 5 * place(r), 5, "arrl")
    g.sem_inc(T.sem.sent, 1)
    wait("y", ("sent", 2))
    e_vec = dm(Y.dma_start(T.vecs[:], T.vec[:]))

    wait("p", c_mK, d2)
    d3 = ev(P.matmul(T.p7[:, 0:1], T.km[:], T.mK[:, 0:1], True, True))
    P.matmul(T.p6[:, 0:16], T.nU[:], T.G[:, 0:16], True, False)
    wait("v", d3)
    d4 = ev(V.tensor_copy(T.ml2[:, 0:1], T.p7[:, 0:1]))
    wait("v", d4, m2)
    d5 = ev(V.tensor_scalar(T.bm[:], T.TB[:, 0:3072].indirect(T.ml2[:, 0:1]), T.mf[:, 1:2], None, A.mult))
    wait("p", d5)
    d6 = ev(P.matmul(T.p6[:, 0:16], T.Ball[:], T.bm[:], False, True))
    wait("v", d6)
    d7 = ev(V.tensor_scalar(T.e2[:], T.p6[:, 0:16], 15.0, None, A.add))
    wait("s", d7, *tb)
    d9 = ev(S.activation(T.kg3[:, 128:256], T.TB[:].indirect(T.e2[:, 8:16]), AF.Copy))
    wait("v", d7)
    d8 = ev(V.tensor_copy(T.kg3[:, 0:128], T.TB[:].indirect(T.e2[:, 0:8])))
    d10 = collect(T.p4, 16, FK, T.kg3, [c_FK, d8, d9])
    wait("v", *e_nk)
    d11 = ev(V.tensor_copy(T.nk2[:], T.nks[:].indirect(T.ml2[:, 0:1])))

    def two_lists(buf, ps, event, add):
        wait("v", event)
        return [ev(V.tensor_scalar(buf[:, 10 * p:10 * p + 10], ps[:, p:20:2], float(add), None, A.add)) for p in range(2)]

    def level(keys, starts, lst, el, ge, bp, ps, deps_v, deps_s):
        wait("s", el[0], *deps_s)
        ea = ev(S.activation(bp[:, 64:160], starts.indirect(lst[:, 4:10]), AF.Copy))
        wait("v", el[0], *deps_v, *deps_s)
        eb = ev(V.tensor_copy(bp[:, 0:64], starts.indirect(lst[:, 0:4])))
        g0 = ev(V.tensor_tensor(ge[:, 0:160], keys.indirect(lst[:, 0:10]), T.X[:, 0:160], A.is_le))
        wait("s", el[1])
        ec = ev(S.activation(bp[:, 160:320], starts.indirect(lst[:, 10:20]), AF.Copy))
        wait("v", el[1])
        g1 = ev(V.tensor_tensor(ge[:, 160:320], keys.indirect(lst[:, 10:20]), T.X[:, 160:320], A.is_le))
        return halves(ps, [(FB, bp, 0, [c_FB, ea, eb]), (F, ge, 0, [g0]), (FB, bp, 1, [ec]), (F, ge, 1, [g1])])

    def child(lst, el, kg, ps):
        ee = []
        for h, va in enumerate((6, 4)):
            c = 10 * h
            wait("s", el[h])
            a = ev(S.activation(kg[:, 16 * (c + va):16 * (c + 10)], T.TB[:].indirect(lst[:, c + va:c + 10]), AF.Copy))
            wait("v", el[h])
            b = ev(V.tensor_copy(kg[:, 16 * c:16 * (c + va)], T.TB[:].indirect(lst[:, c:c + va])))
            ee.append([a, b])
        return halves(ps, [(FK, kg, 0, [c_FK] + ee[0]), (FK, kg, 1, ee[1])])

    wait("v", d11, x_own, s2b)
    w2 = [ev(V.tensor_tensor(T.ge2[:, 240:320], T.nk2[:].indirect(T.s2b[:, 0:5]), T.X[:, 240:320], A.is_le))]
    wait("v", a_x, a_l)
    w2.append(ev(V.tensor_tensor(T.ge2[:, 0:240], T.nk2[:].indirect(T.s2a[:, 0:15]), T.X[:, 0:240], A.is_le)))
    s2f = together([V.tensor_scalar(T.s2f[:, 0:15], T.s2a[:, 0:15], 16.0, None, A.mult),
                    V.tensor_scalar(T.s2f[:, 15:20], T.s2b[:, 0:5], 16.0, None, A.mult)])
    collect(T.p6, 20, F, T.ge2, w2 + [d7, s2], False)
    wait("p", s2f)
    q2 = ev(P.matmul(T.p6[:, 0:20], T.Id[:], T.s2f[:, 0:20], False, True))
    wait("v", d10)
    d12 = ev(V.tensor_copy(T.ml3[:], T.p4[:, 0:16]))
    wait("s", d12)
    d14 = ev(S.activation(T.bl3[:], T.TB[:, 0:3072].indirect(T.ml3[:]), AF.Copy))
    wait("v", d12)
    d13 = ev(V.tensor_copy(T.nk3[:], T.nks[:].indirect(T.ml3[:])))
    wait("v", q2)
    s3 = ev(V.tensor_scalar(T.s3[:], T.p6[:, 0:20], -1.0, None, A.add))
    e3 = two_lists(T.e3, T.p4, level(T.nk3[:], T.bl3[:], T.s3, [s3, s3], T.ge3, T.bp3, T.p4, [d13], [d14]), -1)
    n4 = two_lists(T.n4, T.p5, child(T.e3, e3, T.kg4, T.p5), 0)
    e4 = two_lists(T.e4, T.p6, level(T.nks[:], T.TB[:, 0:3072], T.n4, n4, T.ge4, T.bp4, T.p6, [], []), -1)
    n5 = two_lists(T.n5, T.p4, child(T.e4, e4, T.kg5, T.p4), 0)
    e5 = two_lists(T.e5, T.p5, level(T.nks[:], T.TB[:, 0:3072], T.n5, n5, T.ge5, T.bp5, T.p5, [], []), -1)
    vl = two_lists(T.vl, T.p6, child(T.e5, e5, T.kg6, T.p6), 0)

    wait("v", e_vec, vl[0])
    va = ev(V.tensor_copy(T.An[:, 0:128], T.vecs[:].indirect(T.vl[:, 0:8])))
    wait("s", e_vec, *vl)
    vb = ev(S.activation(T.An[:, 128:256], T.vecs[:].indirect(T.vl[:, 8:16]), AF.Copy))
    wait("v", vl[1])
    vc = ev(V.tensor_copy(T.An[:, 256:320], T.vecs[:].indirect(T.vl[:, 16:20])))
    wait("g", va, vb)
    a_y = send(T.An, lambda r: CAP * ((r - own) % N - 1), T.R, lambda r: CAP * own, CAP, "arry")

    wait("v", ("pl", 32))
    g_t = ev(V.transpose(T.pt[:], T.pg[:]))
    wait("v", vb, vc)
    y0 = ev(V.tensor_copy(T.R[:, CAP * own:CAP * own + CAP], T.An[:, 240:320]))
    wait("v", g_t)
    r_posg = ev(V.tensor_copy(T.posG[:], T.pt[:, 0:16]))
    wait("v", a_y, y0, r_posg)
    wait("s", a_y, y0, r_posg)
    y1 = ev(V.tensor_copy(T.yb[:, 0:128], T.R[:].indirect(T.posG[:, 0:8])))
    y2 = ev(S.activation(T.yb[:, 128:256], T.R[:].indirect(T.posG[:, 8:16]), AF.Copy))
    wait("y", y1, y2)
    st = dm(Y.dma_start(T.y[:], T.yb[:]))
    wait("y", st)
    wait("g", ("left", 48))
